import numpy as np
import ml_dtypes


def mxq(x, axis, fmt="e4m3"):
    dtype, down = {"e4m3": (ml_dtypes.float8_e4m3fn, 7), "e5m2": (ml_dtypes.float8_e5m2, 14)}[fmt]
    v = np.moveaxis(np.asarray(x, np.float32).astype(ml_dtypes.bfloat16).astype(np.float64), axis, -1)
    blocks = v.reshape(v.shape[:-1] + (-1, 32))
    amax = np.abs(blocks).max(-1, keepdims=True)
    byte = np.maximum(np.where(amax > 0, np.frexp(amax)[1] - 1 + 127, 0) - down, 1)
    scale = np.exp2(byte - 127.0)
    codes = (blocks / scale).astype(np.float32).astype(dtype).astype(np.float64)
    return np.moveaxis((codes * scale).reshape(v.shape), -1, axis)


WIDE = False


def mx_kscale(k):
    if not WIDE:
        return np.ones(k)
    levels = np.array([10, -10, 5, -5, 0])
    if k % 512:
        return np.exp2(np.random.permutation(np.resize(levels, k // 32))).repeat(32)
    a = np.empty((k // 512, 16))
    for p in range(k // 512):
        a[p, :8] = np.random.permutation(np.resize(levels, 8))
        for g in range(8):
            far = levels[np.abs(levels - a[p, g]) >= 10]
            a[p, g + 8] = far[np.random.randint(len(far))]
    return np.exp2(a.ravel()).repeat(32)


def f64(x):
    return np.asarray(x).astype(np.float64)


def striped(idx):
    return np.tile(np.asarray(idx).reshape(-1, 16).T, (8, 1)).astype(np.uint16)


def unstriped(offs):
    return offs[:16].T.reshape(-1).astype(np.int64)


E2M1 = np.array([0.0, 0.5, 1.0, 1.5, 2.0, 3.0, 4.0, 6.0, -0.0, -0.5, -1.0, -1.5, -2.0, -3.0, -4.0, -6.0])


def pack_weight(w, fmt):
    k, n = w.shape
    w = f64(np.asarray(w, np.float32).astype(ml_dtypes.bfloat16)).reshape(k // 32, 32, n)
    amax = np.abs(w).max(1)
    if fmt == "e4m3":
        byte = np.frexp(amax)[1] - 1 + 127 - 7
    else:
        mant, ex = np.frexp(amax / 6.0)
        byte = np.where(mant > 0.5, ex, ex - 1) + 127
    byte = np.clip(np.where(amax > 0, byte, 1), 1, 254)
    scaled = (w * np.exp2(127.0 - byte)[:, None, :]).reshape(k, n).astype(np.float32)
    by_word = np.ascontiguousarray(scaled.reshape(k // 512, 128, 4, n).transpose(0, 1, 3, 2))
    if fmt == "e4m3":
        words = by_word.astype(ml_dtypes.float8_e4m3fn).view(np.uint8)
    else:
        c = by_word.astype(ml_dtypes.float4_e2m1fn).view(np.uint8) & 0xF
        words = (c[..., 0::2] | (c[..., 1::2] << 4)).reshape(k // 512, 128, 2 * n)
    return np.ascontiguousarray(words), np.ascontiguousarray(byte.astype(np.uint8).reshape(k // 512, 16, n))


def unpack_weight(words, scales, fmt):
    g, _, n = scales.shape
    words = np.ascontiguousarray(words).reshape(g, 128, n, -1)
    if fmt == "e4m3":
        vals = words.view(ml_dtypes.float8_e4m3fn).astype(np.float64)
    else:
        nib = np.empty((g, 128, n, 4), np.uint8)
        nib[..., 0::2] = words & 0xF
        nib[..., 1::2] = words >> 4
        vals = E2M1[nib]
    vals = vals * np.repeat(np.exp2(scales.astype(np.float64) - 127.0), 8, axis=1)[..., None]
    return vals.transpose(0, 1, 3, 2).reshape(g * 512, n)


def bf(x):
    return np.asarray(x, np.float32).astype(ml_dtypes.bfloat16)


def planes(Y):
    r, m = Y.shape
    b = f64(bf(Y)).reshape(r // 32, 32, m)
    amax = np.abs(b).max(1)
    byte = np.clip(np.where(amax > 0, np.frexp(amax)[1] - 1 + 127 - 7, 1), 1, 254)
    codes = (b * np.exp2(127.0 - byte)[:, None, :]).reshape(r, m).astype(np.float32).astype(ml_dtypes.float8_e4m3fn).view(np.uint8)
    words = codes.reshape(r // 512, 128, 4, m).transpose(0, 1, 3, 2)
    return np.ascontiguousarray(words), np.ascontiguousarray(byte.astype(np.uint8).reshape(r // 512, 16, m))


D, T, I, Q, E, Z = 512, 2048, 512, 256, 512, 1024


def setup_inputs():
    n = np.random.standard_normal
    idx = np.random.permutation(T)[:I]
    idx2 = np.random.permutation(Z)[:I]
    idx3 = np.random.permutation(Z)[:I]
    fd = mx_kscale(D)
    fi = mx_kscale(I)
    ti = np.ones(T)
    ti[idx] = fi
    keysp = pack_weight(n((D, T)) / fd[:, None], "e2m1")
    return {
        "query": (n((D, Q)) * 1.0 / np.sqrt(D) * fd[:, None]).astype(np.float32),
        "keys_words": keysp[0],
        "keys_scales": keysp[1],
        "os": (np.random.uniform(0.02, 0.08, (1, I)) * fi).astype(np.float32),
        "vals": (n((E, T)) / ti).astype(np.float32),
        "offs": striped(idx),
        "offs2": striped(idx2),
        "offs3": striped(idx3),
    }


def reference(query, keys_words, keys_scales, os, vals, offs, offs2, offs3):
    idx = unstriped(offs)
    idx2 = unstriped(offs2)
    idx3 = unstriped(offs3)
    keysu = unpack_weight(keys_words, keys_scales, "e2m1")
    queryq = mxq(f64(query), 0, "e4m3")
    keysidxg = keysu[:, idx]
    a = queryq.T @ keysidxg
    f0 = np.zeros((Q, Z))
    f0[:, idx2] = a
    s = a + f0[:, idx3]
    w = np.maximum(s, 0.0)
    wo1 = w * f64(os)
    wt1 = wo1.T
    vt1 = f64(vals)[:, idx].T
    vt1q = mxq(vt1, 0, "e4m3")
    wt1q = mxq(wt1, 0, "e4m3")
    o = vt1q.T @ wt1q
    words, scales = planes(o)
    return o, words, scales

@@ -1,0 +1,170 @@
+from contextlib import ExitStack
+
+import concourse.mybir as mybir
+from concourse.masks import make_identity
+
+D, T, I, Q, E, Z = 512, 2048, 512, 256, 512, 1024
+FLOPS = 2 * D * Q * I + 2 * I * E * Q
+
+F32 = mybir.dt.float32
+BF16 = mybir.dt.bfloat16
+I32 = mybir.dt.int32
+U32 = mybir.dt.uint32
+U16 = mybir.dt.uint16
+U8 = mybir.dt.uint8
+FP8X4 = mybir.dt.float8_e4m3fn_x4
+FP4X4 = mybir.dt.float4_e2m1fn_x4
+ALU = mybir.AluOpType
+COPY = mybir.ActivationFunctionType.Copy
+
+P = 128
+PACK = 4
+HALVES = Q // P
+
+
+def tile_attend_passedthrough_read_lean_pl_kernel(
+    tc, query, keys_words, keys_scales, slot_factor, vals, offs, offs2, offs3, out_0, out_1, out_2
+):
+    nc = tc.nc
+    with ExitStack() as ctx:
+        sb = ctx.enter_context(tc.tile_pool(name="sb", bufs=1))
+        ps = ctx.enter_context(tc.psum_pool(name="ps", bufs=1))
+
+        def tile(shape, dtype, name):
+            return sb.tile(shape, dtype, name=name, align_bytes=64)
+
+        key_list = tile([P, I // 16], U16, "key_list")
+        put_list = tile([P, I // 16], U16, "put_list")
+        get_list = tile([P, I // 16], U16, "get_list")
+        key_words = tile([P, T], U16, "key_words")
+        key_scales = tile([P, T], U8, "key_scales")
+        q_raw = tile([P, PACK, Q], F32, "q_raw")
+        os_cols = tile([P, PACK], F32, "os_cols")
+        val_pool = [tile([P, T], F32, "val_pool%d" % t) for t in range(PACK)]
+        places = [tile([P, Z], F32, "places%d" % h) for h in range(HALVES)]
+        ident = tile([P, P], F32, "ident")
+
+        nc.vector.memset(key_scales[:].bitcast(I32), 0)
+        vals_by_place = vals.rearrange("(p t) c -> t p c", t=PACK)
+        nc.sync.dma_start(key_list[:], offs)
+        nc.sync.dma_start(key_words[:].bitcast(I32), keys_words[0].bitcast(I32))
+        nc.sync.dma_start(q_raw[:], query.rearrange("(p t) q -> p t q", t=PACK))
+        for g in range(4):
+            nc.scalar.dma_start(
+                key_scales[32 * g : 32 * g + 4, :].bitcast(I32), keys_scales[0, 4 * g : 4 * g + 4, :].bitcast(I32)
+            )
+        nc.sync.dma_start(val_pool[0][:], vals_by_place[0])
+        nc.sync.dma_start(put_list[:], offs2)
+        nc.sync.dma_start(val_pool[1][:], vals_by_place[1])
+        nc.sync.dma_start(get_list[:], offs3)
+        nc.sync.dma_start(os_cols[:], slot_factor.rearrange("o (p t) -> p (o t)", t=PACK))
+        nc.sync.dma_start(val_pool[2][:], vals_by_place[2])
+        nc.sync.dma_start(val_pool[3][:], vals_by_place[3])
+        for h in range(HALVES):
+            nc.vector.memset(places[h][:], 0.0)
+        make_identity(nc, ident[:])
+
+        k_words = tile([P, I], U16, "k_words")
+        k_scales = tile([P, I], U8, "k_scales")
+        nc.vector.tensor_copy(k_words[:], key_words[:].indirect(key_list[:]))
+        nc.vector.tensor_copy(k_scales[:], key_scales[:].indirect(key_list[:]))
+
+        q_bf = tile([P, Q, PACK], BF16, "q_bf")
+        nc.scalar.copy(
+            q_bf[:].rearrange("p (c i) t -> p c t i", i=4), q_raw[:].rearrange("p t (c i) -> p c t i", i=4)
+        )
+        q_codes = tile([P, Q], U32, "q_codes")
+        q_scales = tile([P, Q], U8, "q_scales")
+        nc.vector.quantize_mx(q_codes[:].bitcast(FP8X4), q_scales[:], q_bf[:].rearrange("p q t -> p (q t)"))
+
+        a = []
+        for h in range(HALVES):
+            cols = slice(h * P, (h + 1) * P)
+            a_ps = ps.tile([P, I], F32, name="a_ps%d" % h)
+            nc.tensor.matmul_mx(
+                a_ps[:], q_codes[:, cols].bitcast(FP8X4), q_scales[:, cols], k_words[:].bitcast(FP4X4), k_scales[:],
+                start=True, stop=True,
+            )
+            a_sb = tile([P, I], F32, "a_sb%d" % h)
+            if h == 0:
+                nc.vector.tensor_copy(a_sb[:], a_ps[:])
+            else:
+                nc.scalar.copy(a_sb[:], a_ps[:])
+            a.append(a_sb)
+
+        nc.vector.tensor_copy(places[0][:].indirect(put_list[:]), a[0][:])
+        for part in range(2):
+            nc.scalar.activation(
+                places[1][:].indirect(put_list[:, 16 * part : 16 * part + 16]),
+                a[1][:, 256 * part : 256 * part + 256],
+                COPY,
+            )
+
+        v_codes, v_scales = [], []
+
+        def values(t):
+            v_bf = tile([P, I], BF16, "v_bf%d" % t)
+            nc.scalar.activation(v_bf[:], val_pool[t][:].indirect(key_list[:]), COPY)
+            pairs = v_bf[:].bitcast(F32)
+            v_ps = ps.tile([P, 2, P], F32, name="v_ps", tag="v_ps", bufs=2)
+            for u in range(2):
+                nc.tensor.transpose(v_ps[:, u, :], pairs[:, u::2], ident[:])
+            v_in = tile([P, P, PACK], BF16, "v_in%d" % t)
+            nc.scalar.copy(v_in[:].bitcast(F32), v_ps[:].rearrange("p u m -> p m u"))
+            codes = tile([P, P], U32, "v_codes%d" % t)
+            scales = tile([P, P], U8, "v_scales%d" % t)
+            nc.vector.quantize_mx(codes[:].bitcast(FP8X4), scales[:], v_in[:].rearrange("p m t -> p (m t)"))
+            v_codes.append(codes)
+            v_scales.append(scales)
+
+        w_codes, w_scales = [], []
+
+        def weights(h):
+            s = tile([P, I], F32, "s%d" % h)
+            nc.vector.tensor_tensor(s[:], places[h][:].indirect(get_list[:]), a[h][:], ALU.add)
+            s_ps = ps.tile([P, PACK, P], F32, name="s_ps%d" % h)
+            for t in range(PACK):
+                nc.tensor.transpose(s_ps[:, t, :], s[:, t::PACK], ident[:])
+            w_in = tile([P, P, PACK], BF16, "w_in%d" % h)
+            nc.vector.scalar_tensor_tensor(
+                w_in[:], s_ps[:].rearrange("p t q -> p q t"), 0.0,
+                os_cols[:].unsqueeze(1).to_broadcast([P, P, PACK]), ALU.max, ALU.mult,
+            )
+            codes = tile([P, P], U32, "w_codes%d" % h)
+            scales = tile([P, P], U8, "w_scales%d" % h)
+            nc.vector.quantize_mx(codes[:].bitcast(FP8X4), scales[:], w_in[:].rearrange("p q t -> p (q t)"))
+            w_codes.append(codes)
+            w_scales.append(scales)
+
+        values(0)
+        weights(0)
+        values(1)
+        weights(1)
+        values(2)
+        values(3)
+
+        o_codes = tile([P, Q], U32, "o_codes")
+        o_scales = tile([P, Q], U8, "o_scales")
+        out_rows = out_0.rearrange("(p t) q -> p t q", t=PACK)
+        out_words = out_1[0].rearrange("p c r -> p (c r)").bitcast(I32)
+        for h in range(HALVES):
+            cols = slice(h * P, (h + 1) * P)
+            o_ps = ps.tile([P, PACK, P], F32, name="o_ps%d" % h)
+            for t in range(PACK):
+                nc.tensor.matmul_mx(
+                    o_ps[:, t, :], v_codes[t][:].bitcast(FP8X4), v_scales[t][:],
+                    w_codes[h][:].bitcast(FP8X4), w_scales[h][:], start=True, stop=True,
+                )
+            o_bf = tile([P, P, PACK], BF16, "o_bf%d" % h)
+            nc.vector.tensor_copy(o_bf[:], o_ps[:].rearrange("p t q -> p q t"))
+            o_sb = tile([P, PACK, P], F32, "o_sb%d" % h)
+            nc.scalar.copy(o_sb[:], o_ps[:])
+            nc.vector.quantize_mx(
+                o_codes[:, cols].bitcast(FP8X4), o_scales[:, cols], o_bf[:].rearrange("p q t -> p (q t)")
+            )
+            nc.scalar.dma_start(out_rows[:, :, cols], o_sb[:])
+            nc.sync.dma_start(out_words[:, cols], o_codes[:, cols].bitcast(I32))
+        for g in range(4):
+            nc.sync.dma_start(
+                out_2[0, 4 * g : 4 * g + 4, :].bitcast(I32), o_scales[32 * g : 32 * g + 4, :].bitcast(I32)
+            )

@@ -20,6 +20,10 @@ COPY = mybir.ActivationFunctionType.Copy
 P = 128
 PACK = 4
 HALVES = Q // P
+PART = I // 2
+SPLIT = 320
+POOL_BYTES = 4 * T
+STAGE = PACK * POOL_BYTES
 
 
 def tile_attend_passedthrough_read_lean_pl_kernel(
@@ -28,143 +32,201 @@ def tile_attend_passedthrough_read_lean_pl_kernel(
     nc = tc.nc
     with ExitStack() as ctx:
         sb = ctx.enter_context(tc.tile_pool(name="sb", bufs=1))
+        shared = ctx.enter_context(tc.tile_pool(name="shared", bufs=1))
         ps = ctx.enter_context(tc.psum_pool(name="ps", bufs=1))
 
         def tile(shape, dtype, name):
             return sb.tile(shape, dtype, name=name, align_bytes=64)
+
+        def tile_at(offset, shape, dtype, name):
+            return shared.tile(shape, dtype, name=name, align_bytes=64, offset=offset)
+
+        def bank(tag, shape, name):
+            return ps.tile(shape, F32, name=name, tag=tag)
+
+        def part_of(lst, part):
+            return lst[:, part * PART // 16 : (part + 1) * PART // 16]
 
         key_list = tile([P, I // 16], U16, "key_list")
         put_list = tile([P, I // 16], U16, "put_list")
         get_list = tile([P, I // 16], U16, "get_list")
         key_words = tile([P, T], U16, "key_words")
         key_scales = tile([P, T], U8, "key_scales")
-        q_raw = tile([P, PACK, Q], F32, "q_raw")
-        os_cols = tile([P, PACK], F32, "os_cols")
-        val_pool = [tile([P, T], F32, "val_pool%d" % t) for t in range(PACK)]
+        q_raw = [tile([P, PACK, P], F32, "q_raw%d" % h) for h in range(HALVES)]
+        factor = tile([P, PACK], F32, "factor")
+        val_pool = [tile_at(t * POOL_BYTES, [P, T], F32, "val_pool%d" % t) for t in range(PACK)]
         places = [tile([P, Z], F32, "places%d" % h) for h in range(HALVES)]
         ident = tile([P, P], F32, "ident")
 
         nc.vector.memset(key_scales[:].bitcast(I32), 0)
         vals_by_place = vals.rearrange("(p t) c -> t p c", t=PACK)
+        query_rows = query.rearrange("(p t) q -> p t q", t=PACK)
         nc.sync.dma_start(key_list[:], offs)
         nc.sync.dma_start(key_words[:].bitcast(I32), keys_words[0].bitcast(I32))
-        nc.sync.dma_start(q_raw[:], query.rearrange("(p t) q -> p t q", t=PACK))
         for g in range(4):
-            nc.scalar.dma_start(
+            nc.sync.dma_start(
                 key_scales[32 * g : 32 * g + 4, :].bitcast(I32), keys_scales[0, 4 * g : 4 * g + 4, :].bitcast(I32)
             )
-        nc.sync.dma_start(val_pool[0][:], vals_by_place[0])
+        for h in range(HALVES):
+            nc.sync.dma_start(q_raw[h][:], query_rows[:, :, h * P : (h + 1) * P])
         nc.sync.dma_start(put_list[:], offs2)
+        nc.sync.dma_start(val_pool[0][:], vals_by_place[0])
         nc.sync.dma_start(val_pool[1][:], vals_by_place[1])
         nc.sync.dma_start(get_list[:], offs3)
-        nc.sync.dma_start(os_cols[:], slot_factor.rearrange("o (p t) -> p (o t)", t=PACK))
+        nc.sync.dma_start(factor[:], slot_factor.rearrange("o (p t) -> p (o t)", t=PACK))
         nc.sync.dma_start(val_pool[2][:], vals_by_place[2])
         nc.sync.dma_start(val_pool[3][:], vals_by_place[3])
         for h in range(HALVES):
             nc.vector.memset(places[h][:], 0.0)
         make_identity(nc, ident[:])
 
-        k_words = tile([P, I], U16, "k_words")
-        k_scales = tile([P, I], U8, "k_scales")
-        nc.vector.tensor_copy(k_words[:], key_words[:].indirect(key_list[:]))
-        nc.vector.tensor_copy(k_scales[:], key_scales[:].indirect(key_list[:]))
-
-        q_bf = tile([P, Q, PACK], BF16, "q_bf")
-        nc.scalar.copy(
-            q_bf[:].rearrange("p (c i) t -> p c t i", i=4), q_raw[:].rearrange("p t (c i) -> p c t i", i=4)
-        )
-        q_codes = tile([P, Q], U32, "q_codes")
-        q_scales = tile([P, Q], U8, "q_scales")
-        nc.vector.quantize_mx(q_codes[:].bitcast(FP8X4), q_scales[:], q_bf[:].rearrange("p q t -> p (q t)"))
-
-        a = []
-        for h in range(HALVES):
-            cols = slice(h * P, (h + 1) * P)
-            a_ps = ps.tile([P, I], F32, name="a_ps%d" % h)
-            nc.tensor.matmul_mx(
-                a_ps[:], q_codes[:, cols].bitcast(FP8X4), q_scales[:, cols], k_words[:].bitcast(FP4X4), k_scales[:],
-                start=True, stop=True,
-            )
-            a_sb = tile([P, I], F32, "a_sb%d" % h)
-            if h == 0:
-                nc.vector.tensor_copy(a_sb[:], a_ps[:])
+        def quantise(name, grouped, offset=None):
+            width = grouped.shape[1]
+            if offset is None:
+                codes = tile([P, width], U32, name + "_codes")
             else:
-                nc.scalar.copy(a_sb[:], a_ps[:])
-            a.append(a_sb)
+                codes = tile_at(offset, [P, width], U32, name + "_codes")
+            scales = tile([P, width], U8, name + "_scales")
+            nc.vector.quantize_mx(codes[:].bitcast(FP8X4), scales[:], grouped[:].rearrange("p c t -> p (c t)"))
+            return codes, scales
 
-        nc.vector.tensor_copy(places[0][:].indirect(put_list[:]), a[0][:])
-        for part in range(2):
+        def round_queries(h):
+            q_bf = tile_at(STAGE + h * 2 * I, [P, P, PACK], BF16, "q_bf%d" % h)
             nc.scalar.activation(
-                places[1][:].indirect(put_list[:, 16 * part : 16 * part + 16]),
-                a[1][:, 256 * part : 256 * part + 256],
-                COPY,
+                q_bf[:].rearrange("p (c i) t -> p c t i", i=4), q_raw[h][:].rearrange("p t (c i) -> p c t i", i=4), COPY
             )
+            return q_bf
 
-        v_codes, v_scales = [], []
+        def gather_keys(part):
+            words = tile_at(STAGE + (1 - part) * 4 * I + I + PART, [P, PART], U16, "k_words%d" % part)
+            scales = tile_at(STAGE + (1 - part) * 4 * I + 3 * I, [P, PART], U8, "k_scales%d" % part)
+            nc.vector.tensor_copy(words[:], key_words[:].indirect(part_of(key_list, part)))
+            nc.vector.tensor_copy(scales[:], key_scales[:].indirect(part_of(key_list, part)))
+            return words, scales
 
-        def values(t):
-            v_bf = tile([P, I], BF16, "v_bf%d" % t)
-            nc.scalar.activation(v_bf[:], val_pool[t][:].indirect(key_list[:]), COPY)
+        def product(dst, q, k):
+            nc.tensor.matmul_mx(dst, q[0][:].bitcast(FP8X4), q[1][:], k[0][:].bitcast(FP4X4), k[1][:], start=True, stop=True)
+
+        def scatter(h, part, on_scalar):
+            window = places[h][:].indirect(part_of(put_list, part))
+            src = a[h][:, part * PART : (part + 1) * PART]
+            if on_scalar:
+                nc.scalar.activation(window, src, COPY)
+            else:
+                nc.vector.tensor_copy(window, src)
+
+        def turn_scores(h, src, first):
+            for t in range(PACK):
+                nc.tensor.matmul(
+                    s_ps[h][:, t, :], src[:, t::PACK], ident[:], is_transpose=True,
+                    start=first and t == 0, stop=(not first) and t == PACK - 1,
+                )
+
+        q_bf = [round_queries(h) for h in range(HALVES)]
+        k = [gather_keys(0)]
+        q = [quantise("q%d" % h, q_bf[h]) for h in range(HALVES)]
+        k.append(gather_keys(1))
+
+        a = [tile([P, I], F32, "a%d" % h) for h in range(HALVES)]
+        s_ps = [bank("s%d" % h, [P, PACK, P], "s_ps%d" % h) for h in range(HALVES)]
+        for h in range(HALVES):
+            a_ps = bank("a%d" % h, [P, PART], "a_ps%d_0" % h)
+            product(a_ps[:], q[h], k[0])
+            nc.scalar.copy(a[h][:, 0:PART], a_ps[:])
+        scatter(0, 0, True)
+        scatter(1, 0, False)
+        for h in range(HALVES):
+            a_ps = bank("a%d" % h, [P, PART], "a_ps%d_1" % h)
+            product(a_ps[:], q[h], k[1])
+            if h == 0:
+                nc.scalar.copy(a[h][:, PART:I], a_ps[:])
+            else:
+                nc.vector.tensor_copy(a[h][:, PART:I], a_ps[:])
+        for h in range(HALVES):
+            scatter(h, 1, True)
+        for h in range(HALVES):
+            turn_scores(h, a[h], True)
+
+        v_bf = [tile([P, I], BF16, "v_bf%d" % t) for t in range(PACK)]
+
+        def gather_values(t, first, last, on_scalar):
+            picked = val_pool[t][:].indirect(key_list[:, first // 16 : last // 16])
+            if on_scalar:
+                nc.scalar.activation(v_bf[t][:, first:last], picked, COPY)
+            else:
+                nc.vector.tensor_copy(v_bf[t][:, first:last], picked)
+
+        def turn_values(v_bf, v_ps):
             pairs = v_bf[:].bitcast(F32)
-            v_ps = ps.tile([P, 2, P], F32, name="v_ps", tag="v_ps", bufs=2)
             for u in range(2):
                 nc.tensor.transpose(v_ps[:, u, :], pairs[:, u::2], ident[:])
-            v_in = tile([P, P, PACK], BF16, "v_in%d" % t)
-            nc.scalar.copy(v_in[:].bitcast(F32), v_ps[:].rearrange("p u m -> p m u"))
-            codes = tile([P, P], U32, "v_codes%d" % t)
-            scales = tile([P, P], U8, "v_scales%d" % t)
-            nc.vector.quantize_mx(codes[:].bitcast(FP8X4), scales[:], v_in[:].rearrange("p m t -> p (m t)"))
-            v_codes.append(codes)
-            v_scales.append(scales)
 
-        w_codes, w_scales = [], []
+        def look_up(h):
+            found = tile_at(POOL_BYTES + h * 4 * I, [P, I], F32, "found%d" % h)
+            nc.vector.tensor_copy(found[:], places[h][:].indirect(get_list[:]))
+            turn_scores(h, found, False)
 
-        def weights(h):
-            s = tile([P, I], F32, "s%d" % h)
-            nc.vector.tensor_tensor(s[:], places[h][:].indirect(get_list[:]), a[h][:], ALU.add)
-            s_ps = ps.tile([P, PACK, P], F32, name="s_ps%d" % h)
-            for t in range(PACK):
-                nc.tensor.transpose(s_ps[:, t, :], s[:, t::PACK], ident[:])
-            w_in = tile([P, P, PACK], BF16, "w_in%d" % h)
+        def weights(h, w_in):
             nc.vector.scalar_tensor_tensor(
-                w_in[:], s_ps[:].rearrange("p t q -> p q t"), 0.0,
-                os_cols[:].unsqueeze(1).to_broadcast([P, P, PACK]), ALU.max, ALU.mult,
+                w_in[:], s_ps[h][:].rearrange("p t q -> p q t"), 0.0,
+                factor[:].unsqueeze(1).to_broadcast([P, P, PACK]), ALU.max, ALU.mult,
             )
-            codes = tile([P, P], U32, "w_codes%d" % h)
-            scales = tile([P, P], U8, "w_scales%d" % h)
-            nc.vector.quantize_mx(codes[:].bitcast(FP8X4), scales[:], w_in[:].rearrange("p q t -> p (q t)"))
-            w_codes.append(codes)
-            w_scales.append(scales)
 
-        values(0)
-        weights(0)
-        values(1)
-        weights(1)
-        values(2)
-        values(3)
+        def quantise_values(pair, v_in):
+            nc.scalar.copy(
+                v_in[:].bitcast(F32).rearrange("p (t m) u -> p t m u", t=2), v_ps[pair][:].rearrange("p t u m -> p t m u")
+            )
+            codes, scales = quantise("v%d" % pair, v_in)
+            return [(codes[:, j * P : (j + 1) * P], scales[:, j * P : (j + 1) * P]) for j in range(2)]
 
-        o_codes = tile([P, Q], U32, "o_codes")
-        o_scales = tile([P, Q], U8, "o_scales")
+        LAST = 3 * POOL_BYTES
+        v_ps = [bank("v%d" % pair, [P, 2, 2, P], "v_ps%d" % pair) for pair in range(2)]
+        for t in range(2):
+            gather_values(t, 0, I, False)
+            turn_values(v_bf[t], v_ps[0][:, t])
+        look_up(0)
+        look_up(1)
+        gather_values(2, 0, I, True)
+        turn_values(v_bf[2], v_ps[1][:, 0])
+        w_in = [tile([P, P, PACK], BF16, "w_in0")]
+        weights(0, w_in[0])
+        gather_values(3, 0, SPLIT, True)
+        gather_values(3, SPLIT, I, False)
+        turn_values(v_bf[3], v_ps[1][:, 1])
+        w_in.append(tile_at(LAST, [P, P, PACK], BF16, "w_in1"))
+        weights(1, w_in[1])
+        w = [quantise("w0", w_in[0], LAST + 2 * I)]
+        v = quantise_values(0, tile_at(LAST + 4 * I, [P, 2 * P, PACK], BF16, "v_in0"))
+        w.append(quantise("w1", w_in[1]))
+        v.extend(quantise_values(1, tile([P, 2 * P, PACK], BF16, "v_in1")))
+
         out_rows = out_0.rearrange("(p t) q -> p t q", t=PACK)
         out_words = out_1[0].rearrange("p c r -> p (c r)").bitcast(I32)
+        o_codes = tile([P, Q], U32, "o_codes")
+        o_scales = tile([P, Q], U8, "o_scales")
         for h in range(HALVES):
             cols = slice(h * P, (h + 1) * P)
-            o_ps = ps.tile([P, PACK, P], F32, name="o_ps%d" % h)
-            for t in range(PACK):
-                nc.tensor.matmul_mx(
-                    o_ps[:, t, :], v_codes[t][:].bitcast(FP8X4), v_scales[t][:],
-                    w_codes[h][:].bitcast(FP8X4), w_scales[h][:], start=True, stop=True,
-                )
-            o_bf = tile([P, P, PACK], BF16, "o_bf%d" % h)
-            nc.vector.tensor_copy(o_bf[:], o_ps[:].rearrange("p t q -> p q t"))
             o_sb = tile([P, PACK, P], F32, "o_sb%d" % h)
-            nc.scalar.copy(o_sb[:], o_ps[:])
+            for pair in range(2):
+                o_ps = bank([["a0", "a1"], ["o0", "o1"]][h][pair], [P, 2, P], "o_ps%d_%d" % (h, pair))
+                for j in range(2):
+                    t = 2 * pair + j
+                    nc.tensor.matmul_mx(
+                        o_ps[:, j, :], v[t][0][:].bitcast(FP8X4), v[t][1][:],
+                        w[h][0][:].bitcast(FP8X4), w[h][1][:], start=True, stop=True,
+                    )
+                nc.scalar.copy(o_sb[:, 2 * pair : 2 * pair + 2, :], o_ps[:])
+            nc.sync.dma_start(out_rows[:, :, cols], o_sb[:])
+            o_bf = tile([P, P, PACK], BF16, "o_bf%d" % h)
+            nc.vector.tensor_copy(
+                o_bf[:].rearrange("p (c i) t -> p c t i", i=4), o_sb[:].rearrange("p t (c i) -> p c t i", i=4)
+            )
             nc.vector.quantize_mx(
                 o_codes[:, cols].bitcast(FP8X4), o_scales[:, cols], o_bf[:].rearrange("p q t -> p (q t)")
             )
-            nc.scalar.dma_start(out_rows[:, :, cols], o_sb[:])
             nc.sync.dma_start(out_words[:, cols], o_codes[:, cols].bitcast(I32))
         for g in range(4):
-            nc.sync.dma_start(
+            queue = nc.sync if g % 2 else nc.scalar
+            queue.dma_start(
                 out_2[0, 4 * g : 4 * g + 4, :].bitcast(I32), o_scales[32 * g : 32 * g + 4, :].bitcast(I32)
             )

@@ -52,7 +52,7 @@ def tile_attend_passedthrough_read_lean_pl_kernel(
         get_list = tile([P, I // 16], U16, "get_list")
         key_words = tile([P, T], U16, "key_words")
         key_scales = tile([P, T], U8, "key_scales")
-        q_raw = [tile([P, PACK, P], F32, "q_raw%d" % h) for h in range(HALVES)]
+        q_raw = tile([P, PACK, Q], F32, "q_raw")
         factor = tile([P, PACK], F32, "factor")
         val_pool = [tile_at(t * POOL_BYTES, [P, T], F32, "val_pool%d" % t) for t in range(PACK)]
         places = [tile([P, Z], F32, "places%d" % h) for h in range(HALVES)]
@@ -67,8 +67,7 @@ def tile_attend_passedthrough_read_lean_pl_kernel(
             nc.sync.dma_start(
                 key_scales[32 * g : 32 * g + 4, :].bitcast(I32), keys_scales[0, 4 * g : 4 * g + 4, :].bitcast(I32)
             )
-        for h in range(HALVES):
-            nc.sync.dma_start(q_raw[h][:], query_rows[:, :, h * P : (h + 1) * P])
+        nc.sync.dma_start(q_raw[:], query_rows)
         nc.sync.dma_start(put_list[:], offs2)
         nc.sync.dma_start(val_pool[0][:], vals_by_place[0])
         nc.sync.dma_start(val_pool[1][:], vals_by_place[1])
@@ -92,9 +91,12 @@ def tile_attend_passedthrough_read_lean_pl_kernel(
 
         def round_queries(h):
             q_bf = tile_at(STAGE + h * 2 * I, [P, P, PACK], BF16, "q_bf%d" % h)
-            nc.scalar.activation(
-                q_bf[:].rearrange("p (c i) t -> p c t i", i=4), q_raw[h][:].rearrange("p t (c i) -> p c t i", i=4), COPY
-            )
+            dst = q_bf[:].rearrange("p (c i) t -> p c t i", i=4)
+            src = q_raw[:, :, h * P : (h + 1) * P].rearrange("p t (c i) -> p c t i", i=4)
+            if h == 0:
+                nc.vector.tensor_copy(dst, src)
+            else:
+                nc.scalar.activation(dst, src, COPY)
             return q_bf
 
         def gather_keys(part):
@@ -122,8 +124,8 @@ def tile_attend_passedthrough_read_lean_pl_kernel(
                     start=first and t == 0, stop=(not first) and t == PACK - 1,
                 )
 
-        q_bf = [round_queries(h) for h in range(HALVES)]
         k = [gather_keys(0)]
+        q_bf = [round_queries(h) for h in range(HALVES)]
         q = [quantise("q%d" % h, q_bf[h]) for h in range(HALVES)]
         k.append(gather_keys(1))
 
@@ -172,15 +174,16 @@ def tile_attend_passedthrough_read_lean_pl_kernel(
                 factor[:].unsqueeze(1).to_broadcast([P, P, PACK]), ALU.max, ALU.mult,
             )
 
-        def quantise_values(pair, v_in):
+        def quantise_values(name, v_ps, v_in):
+            count = v_ps.shape[1]
             nc.scalar.copy(
-                v_in[:].bitcast(F32).rearrange("p (t m) u -> p t m u", t=2), v_ps[pair][:].rearrange("p t u m -> p t m u")
+                v_in[:].bitcast(F32).rearrange("p (t m) u -> p t m u", t=count), v_ps[:].rearrange("p t u m -> p t m u")
             )
-            codes, scales = quantise("v%d" % pair, v_in)
-            return [(codes[:, j * P : (j + 1) * P], scales[:, j * P : (j + 1) * P]) for j in range(2)]
+            codes, scales = quantise(name, v_in)
+            return [(codes[:, j * P : (j + 1) * P], scales[:, j * P : (j + 1) * P]) for j in range(count)]
 
         LAST = 3 * POOL_BYTES
-        v_ps = [bank("v%d" % pair, [P, 2, 2, P], "v_ps%d" % pair) for pair in range(2)]
+        v_ps = [bank("v%d" % j, [P, count, 2, P], "v_ps%d" % j) for j, count in enumerate((2, 1, 1))]
         for t in range(2):
             gather_values(t, 0, I, False)
             turn_values(v_bf[t], v_ps[0][:, t])
@@ -192,39 +195,45 @@ def tile_attend_passedthrough_read_lean_pl_kernel(
         weights(0, w_in[0])
         gather_values(3, 0, SPLIT, True)
         gather_values(3, SPLIT, I, False)
-        turn_values(v_bf[3], v_ps[1][:, 1])
+        turn_values(v_bf[3], v_ps[2][:, 0])
         w_in.append(tile_at(LAST, [P, P, PACK], BF16, "w_in1"))
         weights(1, w_in[1])
         w = [quantise("w0", w_in[0], LAST + 2 * I)]
-        v = quantise_values(0, tile_at(LAST + 4 * I, [P, 2 * P, PACK], BF16, "v_in0"))
+        v = quantise_values("v01", v_ps[0], tile_at(LAST + 4 * I, [P, 2 * P, PACK], BF16, "v_in01"))
         w.append(quantise("w1", w_in[1]))
-        v.extend(quantise_values(1, tile([P, 2 * P, PACK], BF16, "v_in1")))
+        v.extend(quantise_values("v2", v_ps[1], tile_at(LAST + 8 * I, [P, P, PACK], BF16, "v_in2")))
+        v.extend(quantise_values("v3", v_ps[2], tile([P, P, PACK], BF16, "v_in3")))
 
         out_rows = out_0.rearrange("(p t) q -> p t q", t=PACK)
         out_words = out_1[0].rearrange("p c r -> p (c r)").bitcast(I32)
         o_codes = tile([P, Q], U32, "o_codes")
         o_scales = tile([P, Q], U8, "o_scales")
-        for h in range(HALVES):
-            cols = slice(h * P, (h + 1) * P)
-            o_sb = tile([P, PACK, P], F32, "o_sb%d" % h)
-            for pair in range(2):
-                o_ps = bank([["a0", "a1"], ["o0", "o1"]][h][pair], [P, 2, P], "o_ps%d_%d" % (h, pair))
+        o_sb = [tile([P, PACK, P], F32, "o_sb%d" % h) for h in range(HALVES)]
+        for pair in range(2):
+            rows = slice(2 * pair, 2 * pair + 2)
+            for h in range(HALVES):
+                o_ps = bank(["a%d", "s%d"][pair] % h, [P, 2, P], "o_ps%d_%d" % (h, pair))
                 for j in range(2):
                     t = 2 * pair + j
                     nc.tensor.matmul_mx(
                         o_ps[:, j, :], v[t][0][:].bitcast(FP8X4), v[t][1][:],
                         w[h][0][:].bitcast(FP8X4), w[h][1][:], start=True, stop=True,
                     )
-                nc.scalar.copy(o_sb[:, 2 * pair : 2 * pair + 2, :], o_ps[:])
-            nc.sync.dma_start(out_rows[:, :, cols], o_sb[:])
+                nc.scalar.copy(o_sb[h][:, rows, :], o_ps[:])
+                if h == 1:
+                    nc.sync.dma_start(out_rows[:, rows, P:Q], o_sb[1][:, rows, :])
+                elif pair == 1:
+                    nc.sync.dma_start(out_rows[:, :, 0:P], o_sb[0][:])
+        for h in range(HALVES):
+            cols = slice(h * P, (h + 1) * P)
             o_bf = tile([P, P, PACK], BF16, "o_bf%d" % h)
             nc.vector.tensor_copy(
-                o_bf[:].rearrange("p (c i) t -> p c t i", i=4), o_sb[:].rearrange("p t (c i) -> p c t i", i=4)
+                o_bf[:].rearrange("p (c i) t -> p c t i", i=4), o_sb[h][:].rearrange("p t (c i) -> p c t i", i=4)
             )
             nc.vector.quantize_mx(
                 o_codes[:, cols].bitcast(FP8X4), o_scales[:, cols], o_bf[:].rearrange("p q t -> p (q t)")
             )
-            nc.sync.dma_start(out_words[:, cols], o_codes[:, cols].bitcast(I32))
+        nc.sync.dma_start(out_words, o_codes[:].bitcast(I32))
         for g in range(4):
             queue = nc.sync if g % 2 else nc.scalar
             queue.dma_start(

@@ -21,7 +21,6 @@ P = 128
 PACK = 4
 HALVES = Q // P
 PART = I // 2
-SPLIT = 320
 POOL_BYTES = 4 * T
 STAGE = PACK * POOL_BYTES
 
@@ -140,10 +139,7 @@ def tile_attend_passedthrough_read_lean_pl_kernel(
         for h in range(HALVES):
             a_ps = bank("a%d" % h, [P, PART], "a_ps%d_1" % h)
             product(a_ps[:], q[h], k[1])
-            if h == 0:
-                nc.scalar.copy(a[h][:, PART:I], a_ps[:])
-            else:
-                nc.vector.tensor_copy(a[h][:, PART:I], a_ps[:])
+            nc.scalar.copy(a[h][:, PART:I], a_ps[:])
         for h in range(HALVES):
             scatter(h, 1, True)
         for h in range(HALVES):
@@ -151,12 +147,12 @@ def tile_attend_passedthrough_read_lean_pl_kernel(
 
         v_bf = [tile([P, I], BF16, "v_bf%d" % t) for t in range(PACK)]
 
-        def gather_values(t, first, last, on_scalar):
-            picked = val_pool[t][:].indirect(key_list[:, first // 16 : last // 16])
+        def gather_values(t, on_scalar):
+            picked = val_pool[t][:].indirect(key_list[:])
             if on_scalar:
-                nc.scalar.activation(v_bf[t][:, first:last], picked, COPY)
+                nc.scalar.activation(v_bf[t][:], picked, COPY)
             else:
-                nc.vector.tensor_copy(v_bf[t][:, first:last], picked)
+                nc.vector.tensor_copy(v_bf[t][:], picked)
 
         def turn_values(v_bf, v_ps):
             pairs = v_bf[:].bitcast(F32)
@@ -174,35 +170,39 @@ def tile_attend_passedthrough_read_lean_pl_kernel(
                 factor[:].unsqueeze(1).to_broadcast([P, P, PACK]), ALU.max, ALU.mult,
             )
 
-        def quantise_values(name, v_ps, v_in):
+        def regroup_values(v_ps, v_in, on_scalar):
             count = v_ps.shape[1]
-            nc.scalar.copy(
-                v_in[:].bitcast(F32).rearrange("p (t m) u -> p t m u", t=count), v_ps[:].rearrange("p t u m -> p t m u")
-            )
-            codes, scales = quantise(name, v_in)
-            return [(codes[:, j * P : (j + 1) * P], scales[:, j * P : (j + 1) * P]) for j in range(count)]
+            dst = v_in[:].bitcast(F32).rearrange("p (t m) u -> p t m u", t=count)
+            src = v_ps[:].rearrange("p t u m -> p t m u")
+            if on_scalar:
+                nc.scalar.copy(dst, src)
+            else:
+                nc.vector.tensor_copy(dst, src)
 
         LAST = 3 * POOL_BYTES
         v_ps = [bank("v%d" % j, [P, count, 2, P], "v_ps%d" % j) for j, count in enumerate((2, 1, 1))]
         for t in range(2):
-            gather_values(t, 0, I, False)
+            gather_values(t, False)
             turn_values(v_bf[t], v_ps[0][:, t])
         look_up(0)
         look_up(1)
-        gather_values(2, 0, I, True)
-        turn_values(v_bf[2], v_ps[1][:, 0])
-        w_in = [tile([P, P, PACK], BF16, "w_in0")]
+        v_in01 = tile([P, 2 * P, PACK], BF16, "v_in01")
+        regroup_values(v_ps[0], v_in01, False)
+        for t in range(2, PACK):
+            gather_values(t, True)
+            turn_values(v_bf[t], v_ps[t - 1][:, 0])
+        w_in = [tile([P, P, PACK], BF16, "w_in%d" % h) for h in range(HALVES)]
         weights(0, w_in[0])
-        gather_values(3, 0, SPLIT, True)
-        gather_values(3, SPLIT, I, False)
-        turn_values(v_bf[3], v_ps[2][:, 0])
-        w_in.append(tile_at(LAST, [P, P, PACK], BF16, "w_in1"))
+        codes, scales = quantise("v01", v_in01)
+        v = [(codes[:, j * P : (j + 1) * P], scales[:, j * P : (j + 1) * P]) for j in range(2)]
         weights(1, w_in[1])
-        w = [quantise("w0", w_in[0], LAST + 2 * I)]
-        v = quantise_values("v01", v_ps[0], tile_at(LAST + 4 * I, [P, 2 * P, PACK], BF16, "v_in01"))
-        w.append(quantise("w1", w_in[1]))
-        v.extend(quantise_values("v2", v_ps[1], tile_at(LAST + 8 * I, [P, P, PACK], BF16, "v_in2")))
-        v.extend(quantise_values("v3", v_ps[2], tile([P, P, PACK], BF16, "v_in3")))
+        w = [quantise("w%d" % h, w_in[h], LAST + h * I) for h in range(HALVES)]
+        v_in2 = tile_at(LAST + 2 * I, [P, P, PACK], BF16, "v_in2")
+        regroup_values(v_ps[1], v_in2, True)
+        v.append(quantise("v2", v_in2))
+        v_in3 = tile([P, P, PACK], BF16, "v_in3")
+        regroup_values(v_ps[2], v_in3, True)
+        v.append(quantise("v3", v_in3))
 
         out_rows = out_0.rearrange("(p t) q -> p t q", t=PACK)
         out_words = out_1[0].rearrange("p c r -> p (c r)").bitcast(I32)

from contextlib import ExitStack

import concourse.mybir as mybir
from concourse.masks import make_identity

D, T, I, Q, E, Z = 512, 2048, 512, 256, 512, 1024
FLOPS = 2 * D * Q * I + 2 * I * E * Q

F32 = mybir.dt.float32
BF16 = mybir.dt.bfloat16
I32 = mybir.dt.int32
U32 = mybir.dt.uint32
U16 = mybir.dt.uint16
U8 = mybir.dt.uint8
FP8X4 = mybir.dt.float8_e4m3fn_x4
FP4X4 = mybir.dt.float4_e2m1fn_x4
ALU = mybir.AluOpType
COPY = mybir.ActivationFunctionType.Copy

P = 128
PACK = 4
HALVES = Q // P
PART = I // 2
POOL_BYTES = 4 * T
STAGE = PACK * POOL_BYTES


def tile_attend_passedthrough_read_lean_pl_kernel(
    tc, query, keys_words, keys_scales, slot_factor, vals, offs, offs2, offs3, out_0, out_1, out_2
):
    nc = tc.nc
    with ExitStack() as ctx:
        sb = ctx.enter_context(tc.tile_pool(name="sb", bufs=1))
        shared = ctx.enter_context(tc.tile_pool(name="shared", bufs=1))
        ps = ctx.enter_context(tc.psum_pool(name="ps", bufs=1))

        def tile(shape, dtype, name):
            return sb.tile(shape, dtype, name=name, align_bytes=64)

        def tile_at(offset, shape, dtype, name):
            return shared.tile(shape, dtype, name=name, align_bytes=64, offset=offset)

        def bank(tag, shape, name):
            return ps.tile(shape, F32, name=name, tag=tag)

        def part_of(lst, part):
            return lst[:, part * PART // 16 : (part + 1) * PART // 16]

        key_list = tile([P, I // 16], U16, "key_list")
        put_list = tile([P, I // 16], U16, "put_list")
        get_list = tile([P, I // 16], U16, "get_list")
        key_words = tile([P, T], U16, "key_words")
        key_scales = tile([P, T], U8, "key_scales")
        q_raw = tile([P, PACK, Q], F32, "q_raw")
        factor = tile([P, PACK], F32, "factor")
        val_pool = [tile_at(t * POOL_BYTES, [P, T], F32, "val_pool%d" % t) for t in range(PACK)]
        places = [tile([P, Z], F32, "places%d" % h) for h in range(HALVES)]
        ident = tile([P, P], F32, "ident")

        nc.vector.memset(key_scales[:].bitcast(I32), 0)
        vals_by_place = vals.rearrange("(p t) c -> t p c", t=PACK)
        query_rows = query.rearrange("(p t) q -> p t q", t=PACK)
        nc.sync.dma_start(key_list[:], offs)
        nc.sync.dma_start(key_words[:].bitcast(I32), keys_words[0].bitcast(I32))
        for g in range(4):
            nc.sync.dma_start(
                key_scales[32 * g : 32 * g + 4, :].bitcast(I32), keys_scales[0, 4 * g : 4 * g + 4, :].bitcast(I32)
            )
        nc.sync.dma_start(q_raw[:], query_rows)
        nc.sync.dma_start(put_list[:], offs2)
        nc.sync.dma_start(val_pool[0][:], vals_by_place[0])
        nc.sync.dma_start(val_pool[1][:], vals_by_place[1])
        nc.sync.dma_start(get_list[:], offs3)
        nc.sync.dma_start(factor[:], slot_factor.rearrange("o (p t) -> p (o t)", t=PACK))
        nc.sync.dma_start(val_pool[2][:], vals_by_place[2])
        nc.sync.dma_start(val_pool[3][:], vals_by_place[3])
        for h in range(HALVES):
            nc.vector.memset(places[h][:], 0.0)
        make_identity(nc, ident[:])

        def quantise(name, grouped, offset=None):
            width = grouped.shape[1]
            if offset is None:
                codes = tile([P, width], U32, name + "_codes")
            else:
                codes = tile_at(offset, [P, width], U32, name + "_codes")
            scales = tile([P, width], U8, name + "_scales")
            nc.vector.quantize_mx(codes[:].bitcast(FP8X4), scales[:], grouped[:].rearrange("p c t -> p (c t)"))
            return codes, scales

        def round_queries(h):
            q_bf = tile_at(STAGE + h * 2 * I, [P, P, PACK], BF16, "q_bf%d" % h)
            dst = q_bf[:].rearrange("p (c i) t -> p c t i", i=4)
            src = q_raw[:, :, h * P : (h + 1) * P].rearrange("p t (c i) -> p c t i", i=4)
            if h == 0:
                nc.vector.tensor_copy(dst, src)
            else:
                nc.scalar.activation(dst, src, COPY)
            return q_bf

        def gather_keys(part):
            words = tile_at(STAGE + (1 - part) * 4 * I + I + PART, [P, PART], U16, "k_words%d" % part)
            scales = tile_at(STAGE + (1 - part) * 4 * I + 3 * I, [P, PART], U8, "k_scales%d" % part)
            nc.vector.tensor_copy(words[:], key_words[:].indirect(part_of(key_list, part)))
            nc.vector.tensor_copy(scales[:], key_scales[:].indirect(part_of(key_list, part)))
            return words, scales

        def product(dst, q, k):
            nc.tensor.matmul_mx(dst, q[0][:].bitcast(FP8X4), q[1][:], k[0][:].bitcast(FP4X4), k[1][:], start=True, stop=True)

        def scatter(h, part, on_scalar):
            window = places[h][:].indirect(part_of(put_list, part))
            src = a[h][:, part * PART : (part + 1) * PART]
            if on_scalar:
                nc.scalar.activation(window, src, COPY)
            else:
                nc.vector.tensor_copy(window, src)

        def turn_scores(h, src, first):
            for t in range(PACK):
                nc.tensor.matmul(
                    s_ps[h][:, t, :], src[:, t::PACK], ident[:], is_transpose=True,
                    start=first and t == 0, stop=(not first) and t == PACK - 1,
                )

        k = [gather_keys(0)]
        q_bf = [round_queries(h) for h in range(HALVES)]
        q = [quantise("q%d" % h, q_bf[h]) for h in range(HALVES)]
        k.append(gather_keys(1))

        a = [tile([P, I], F32, "a%d" % h) for h in range(HALVES)]
        s_ps = [bank("s%d" % h, [P, PACK, P], "s_ps%d" % h) for h in range(HALVES)]
        for h in range(HALVES):
            a_ps = bank("a%d" % h, [P, PART], "a_ps%d_0" % h)
            product(a_ps[:], q[h], k[0])
            nc.scalar.copy(a[h][:, 0:PART], a_ps[:])
        scatter(0, 0, True)
        scatter(1, 0, False)
        for h in range(HALVES):
            a_ps = bank("a%d" % h, [P, PART], "a_ps%d_1" % h)
            product(a_ps[:], q[h], k[1])
            nc.scalar.copy(a[h][:, PART:I], a_ps[:])
        for h in range(HALVES):
            scatter(h, 1, True)
        for h in range(HALVES):
            turn_scores(h, a[h], True)

        v_bf = [tile([P, I], BF16, "v_bf%d" % t) for t in range(PACK)]

        def gather_values(t, on_scalar):
            picked = val_pool[t][:].indirect(key_list[:])
            if on_scalar:
                nc.scalar.activation(v_bf[t][:], picked, COPY)
            else:
                nc.vector.tensor_copy(v_bf[t][:], picked)

        def turn_values(v_bf, v_ps):
            pairs = v_bf[:].bitcast(F32)
            for u in range(2):
                nc.tensor.transpose(v_ps[:, u, :], pairs[:, u::2], ident[:])

        def look_up(h):
            found = tile_at(POOL_BYTES + h * 4 * I, [P, I], F32, "found%d" % h)
            nc.vector.tensor_copy(found[:], places[h][:].indirect(get_list[:]))
            turn_scores(h, found, False)

        def weights(h, w_in):
            nc.vector.scalar_tensor_tensor(
                w_in[:], s_ps[h][:].rearrange("p t q -> p q t"), 0.0,
                factor[:].unsqueeze(1).to_broadcast([P, P, PACK]), ALU.max, ALU.mult,
            )

        def regroup_values(v_ps, v_in, on_scalar):
            count = v_ps.shape[1]
            dst = v_in[:].bitcast(F32).rearrange("p (t m) u -> p t m u", t=count)
            src = v_ps[:].rearrange("p t u m -> p t m u")
            if on_scalar:
                nc.scalar.copy(dst, src)
            else:
                nc.vector.tensor_copy(dst, src)

        LAST = 3 * POOL_BYTES
        v_ps = [bank("v%d" % j, [P, count, 2, P], "v_ps%d" % j) for j, count in enumerate((2, 1, 1))]
        for t in range(2):
            gather_values(t, False)
            turn_values(v_bf[t], v_ps[0][:, t])
        look_up(0)
        look_up(1)
        v_in01 = tile([P, 2 * P, PACK], BF16, "v_in01")
        regroup_values(v_ps[0], v_in01, False)
        for t in range(2, PACK):
            gather_values(t, True)
            turn_values(v_bf[t], v_ps[t - 1][:, 0])
        w_in = [tile([P, P, PACK], BF16, "w_in%d" % h) for h in range(HALVES)]
        weights(0, w_in[0])
        codes, scales = quantise("v01", v_in01)
        v = [(codes[:, j * P : (j + 1) * P], scales[:, j * P : (j + 1) * P]) for j in range(2)]
        weights(1, w_in[1])
        w = [quantise("w%d" % h, w_in[h], LAST + h * I) for h in range(HALVES)]
        v_in2 = tile_at(LAST + 2 * I, [P, P, PACK], BF16, "v_in2")
        regroup_values(v_ps[1], v_in2, True)
        v.append(quantise("v2", v_in2))
        v_in3 = tile([P, P, PACK], BF16, "v_in3")
        regroup_values(v_ps[2], v_in3, True)
        v.append(quantise("v3", v_in3))

        out_rows = out_0.rearrange("(p t) q -> p t q", t=PACK)
        out_words = out_1[0].rearrange("p c r -> p (c r)").bitcast(I32)
        o_codes = tile([P, Q], U32, "o_codes")
        o_scales = tile([P, Q], U8, "o_scales")
        o_sb = [tile([P, PACK, P], F32, "o_sb%d" % h) for h in range(HALVES)]
        for pair in range(2):
            rows = slice(2 * pair, 2 * pair + 2)
            for h in range(HALVES):
                o_ps = bank(["a%d", "s%d"][pair] % h, [P, 2, P], "o_ps%d_%d" % (h, pair))
                for j in range(2):
                    t = 2 * pair + j
                    nc.tensor.matmul_mx(
                        o_ps[:, j, :], v[t][0][:].bitcast(FP8X4), v[t][1][:],
                        w[h][0][:].bitcast(FP8X4), w[h][1][:], start=True, stop=True,
                    )
                nc.scalar.copy(o_sb[h][:, rows, :], o_ps[:])
                if h == 1:
                    nc.sync.dma_start(out_rows[:, rows, P:Q], o_sb[1][:, rows, :])
                elif pair == 1:
                    nc.sync.dma_start(out_rows[:, :, 0:P], o_sb[0][:])
        for h in range(HALVES):
            cols = slice(h * P, (h + 1) * P)
            o_bf = tile([P, P, PACK], BF16, "o_bf%d" % h)
            nc.vector.tensor_copy(
                o_bf[:].rearrange("p (c i) t -> p c t i", i=4), o_sb[h][:].rearrange("p t (c i) -> p c t i", i=4)
            )
            nc.vector.quantize_mx(
                o_codes[:, cols].bitcast(FP8X4), o_scales[:, cols], o_bf[:].rearrange("p q t -> p (q t)")
            )
        nc.sync.dma_start(out_words, o_codes[:].bitcast(I32))
        for g in range(4):
            queue = nc.sync if g % 2 else nc.scalar
            queue.dma_start(
                out_2[0, 4 * g : 4 * g + 4, :].bitcast(I32), o_scales[32 * g : 32 * g + 4, :].bitcast(I32)
            )
